import numpy as np
CORES = [66,67,70,71,194,195,198,199]
N = 8
def setup_inputs(rng):
    return {"x1": rng.standard_normal((N, 128, 3), dtype=np.float32), "x2": rng.standard_normal((N, 128, 1), dtype=np.float32), "x3": rng.standard_normal((N, 128, 4), dtype=np.float32), "x4": rng.standard_normal((N, 128, 2), dtype=np.float32)}
def reference(x1, x2, x3, x4):
    out = {}
    s = x1.sum(axis=0, dtype=np.float64).astype(x1.dtype)
    out["y1"] = np.broadcast_to(s, (N,) + s.shape)
    s = x2.sum(axis=0, dtype=np.float64).astype(x2.dtype)
    out["y2"] = np.broadcast_to(s, (N,) + s.shape)
    s = x3.sum(axis=0, dtype=np.float64).astype(x3.dtype)
    out["y3"] = np.broadcast_to(s, (N,) + s.shape)
    s = x4.sum(axis=0, dtype=np.float64).astype(x4.dtype)
    out["y4"] = np.broadcast_to(s, (N,) + s.shape)
    return out

@@ -1,0 +1,67 @@
+from concourse.bass import DstId, RemoteDMATransfer
+
+NB = 5
+PIECE = {3: (0, 256), 1: (256, 448), 2: (448, 512), 4: (512, 640)}
+
+SCRATCH = {
+    "pack": ("dram", [128 * NB, 2], "float32"),
+    "land": ("dram", [8 * NB, 128, 2], "float32"),
+    "res": ("dram", [128 * NB, 2], "float32"),
+}
+SEMAPHORES = ["loaded", "sent", "arrived", "summed", "stored"]
+
+HELPER_CORE = 0
+
+
+def rank_program(g, core, T, topo):
+    cores = list(T.cores)
+    n = len(cores)
+    helpers = sorted(set((c // 8) * 8 + HELPER_CORE for c in cores))
+    rank = T.rank_of(core)
+
+    if core in helpers:
+        mine = [c for c in cores if c // 8 == core // 8]
+        ids = []
+        for c in mine:
+            rid, pid = topo.addr(c, core)
+            ids.append(DstId(rid=rid, pnc=pid))
+        g.wait_ge(T.sem.arrived, n * NB)
+        g.remote_dma_fused(
+            [RemoteDMATransfer(dst_ids=ids, dma_engine_mask=0x3 << (2 * k), remote_sem=T.sem.summed,
+                               srcs=[T.land[r * NB + k] for r in range(n)],
+                               dsts=[T.res[k * 128:(k + 1) * 128, :] for c in mine], alu_op=1)
+             for k in range(NB)],
+            local_sem=T.sem.sent)
+        g.wait_ge(T.sem.sent, 2 * NB)
+        return
+
+    if rank is None:
+        return
+
+    queue = {3: g.sync, 2: g.sync, 1: g.scalar, 4: g.scalar}
+    order = (3, 1, 4, 2)
+
+    for k in order:
+        a, b = PIECE[k]
+        queue[k].dma_start(T.pack[a:b, :], T["x%d" % k][:]).then_inc(T.sem.loaded, 16)
+    g.wait_ge(T.sem.loaded, 64)
+
+    transfers = []
+    for h in sorted(helpers, key=lambda h: h // 8 == core // 8):
+        rid, pid = topo.addr(h, core)
+        base = 0 if h // 8 != core // 8 else 8
+        for k in range(NB):
+            transfers.append(RemoteDMATransfer(dst_ids=[DstId(rid=rid, pnc=pid)], dma_engine_mask=1 << (base + k),
+                                               remote_sem=T.sem.arrived, src=T.pack[k * 128:(k + 1) * 128, :],
+                                               dst=T.land[rank * NB + k]))
+    g.remote_dma_fused(transfers, local_sem=T.sem.sent)
+
+    g.sync.wait_ge(T.sem.summed, 2 * NB)
+    g.scalar.wait_ge(T.sem.summed, 2 * NB)
+    for k in order:
+        a, b = PIECE[k]
+        queue[k].dma_start(T["y%d" % k][:], T.res[a:b, :]).then_inc(T.sem.stored, 16)
+
+    g.wait_ge(T.sem.sent, 2 * NB)
+    g.wait_ge(T.sem.summed, 2 * NB)
+    g.wait_ge(T.sem.stored, 64)

@@ -1,38 +1,46 @@
 from concourse.bass import DstId, RemoteDMATransfer
 
-NB = 5
-PIECE = {3: (0, 256), 1: (256, 448), 2: (448, 512), 4: (512, 640)}
+W = 4
+PIECE = {3: (0, 128), 1: (128, 224), 2: (224, 256), 4: (256, 320)}
+START = (0, 128, 192)
+NB = len(START)
+RES = {3: (0, 128), 1: (128, 224), 2: (224, 256), 4: (320, 384)}
 
 SCRATCH = {
-    "pack": ("dram", [128 * NB, 2], "float32"),
-    "land": ("dram", [8 * NB, 128, 2], "float32"),
-    "res": ("dram", [128 * NB, 2], "float32"),
+    "pack": ("dram", [320, W], "float32"),
+    "land": ("dram", [8 * NB, 128, W], "float32"),
+    "res": ("dram", [128 * NB, W], "float32"),
 }
 SEMAPHORES = ["loaded", "sent", "arrived", "summed", "stored"]
 
-HELPER_CORE = 0
+HELPER_CORES = (0, 4, 1)
+GE = 2
+FE = 4
 
 
 def rank_program(g, core, T, topo):
     cores = list(T.cores)
     n = len(cores)
-    helpers = sorted(set((c // 8) * 8 + HELPER_CORE for c in cores))
     rank = T.rank_of(core)
+    chips = sorted(set(c // 8 for c in cores))
 
-    if core in helpers:
+    def folder(chip8, k):
+        return chip8 * 8 + HELPER_CORES[k]
+
+    blocks = [k for k in range(NB) if core // 8 in chips and folder(core // 8, k) == core]
+    if blocks:
         mine = [c for c in cores if c // 8 == core // 8]
-        ids = []
-        for c in mine:
-            rid, pid = topo.addr(c, core)
-            ids.append(DstId(rid=rid, pnc=pid))
-        g.wait_ge(T.sem.arrived, n * NB)
-        g.remote_dma_fused(
-            [RemoteDMATransfer(dst_ids=ids, dma_engine_mask=0x3 << (2 * k), remote_sem=T.sem.summed,
-                               srcs=[T.land[r * NB + k] for r in range(n)],
-                               dsts=[T.res[k * 128:(k + 1) * 128, :] for c in mine], alu_op=1)
-             for k in range(NB)],
-            local_sem=T.sem.sent)
-        g.wait_ge(T.sem.sent, 2 * NB)
+        folds = []
+        for k in blocks:
+            for c in mine:
+                rid, pid = topo.addr(c, core)
+                folds.append(RemoteDMATransfer(dst_ids=[DstId(rid=rid, pnc=pid)],
+                                               dma_engine_mask=((1 << FE) - 1) << (FE * len(folds)),
+                                               remote_sem=T.sem.summed, srcs=[T.land[r * NB + k] for r in range(n)],
+                                               dsts=[T.res[k * 128:(k + 1) * 128, :]], alu_op=1))
+        g.wait_ge(T.sem.arrived, GE * n * len(blocks))
+        g.remote_dma_fused(folds, local_sem=T.sem.sent)
+        g.wait_ge(T.sem.sent, FE * len(folds))
         return
 
     if rank is None:
@@ -47,21 +55,22 @@ def rank_program(g, core, T, topo):
     g.wait_ge(T.sem.loaded, 64)
 
     transfers = []
-    for h in sorted(helpers, key=lambda h: h // 8 == core // 8):
-        rid, pid = topo.addr(h, core)
-        base = 0 if h // 8 != core // 8 else 8
-        for k in range(NB):
-            transfers.append(RemoteDMATransfer(dst_ids=[DstId(rid=rid, pnc=pid)], dma_engine_mask=1 << (base + k),
-                                               remote_sem=T.sem.arrived, src=T.pack[k * 128:(k + 1) * 128, :],
-                                               dst=T.land[rank * NB + k]))
+    for k in range(NB):
+        ids = []
+        for ch in sorted(chips, key=lambda ch: ch == core // 8):
+            rid, pid = topo.addr(folder(ch, k), core)
+            ids.append(DstId(rid=rid, pnc=pid))
+        transfers.append(RemoteDMATransfer(dst_ids=ids, dma_engine_mask=((1 << GE) - 1) << (GE * k),
+                                           remote_sem=T.sem.arrived, srcs=[T.pack[START[k]:START[k] + 128, :]],
+                                           dsts=[T.land[rank * NB + k] for i in ids]))
     g.remote_dma_fused(transfers, local_sem=T.sem.sent)
 
-    g.sync.wait_ge(T.sem.summed, 2 * NB)
-    g.scalar.wait_ge(T.sem.summed, 2 * NB)
+    g.sync.wait_ge(T.sem.summed, FE * NB)
+    g.scalar.wait_ge(T.sem.summed, FE * NB)
     for k in order:
-        a, b = PIECE[k]
+        a, b = RES[k]
         queue[k].dma_start(T["y%d" % k][:], T.res[a:b, :]).then_inc(T.sem.stored, 16)
 
-    g.wait_ge(T.sem.sent, 2 * NB)
-    g.wait_ge(T.sem.summed, 2 * NB)
+    g.wait_ge(T.sem.sent, GE * NB)
+    g.wait_ge(T.sem.summed, FE * NB)
     g.wait_ge(T.sem.stored, 64)

@@ -15,7 +15,7 @@ SEMAPHORES = ["loaded", "sent", "arrived", "summed", "stored"]
 
 HELPER_CORES = (0, 4, 1)
 GE = 2
-FE = 4
+FE = 16
 
 
 def rank_program(g, core, T, topo):
@@ -30,14 +30,14 @@ def rank_program(g, core, T, topo):
     blocks = [k for k in range(NB) if core // 8 in chips and folder(core // 8, k) == core]
     if blocks:
         mine = [c for c in cores if c // 8 == core // 8]
-        folds = []
-        for k in blocks:
-            for c in mine:
-                rid, pid = topo.addr(c, core)
-                folds.append(RemoteDMATransfer(dst_ids=[DstId(rid=rid, pnc=pid)],
-                                               dma_engine_mask=((1 << FE) - 1) << (FE * len(folds)),
-                                               remote_sem=T.sem.summed, srcs=[T.land[r * NB + k] for r in range(n)],
-                                               dsts=[T.res[k * 128:(k + 1) * 128, :]], alu_op=1))
+        ids = []
+        for c in mine:
+            rid, pid = topo.addr(c, core)
+            ids.append(DstId(rid=rid, pnc=pid))
+        k = blocks[0]
+        folds = [RemoteDMATransfer(dst_ids=ids, dma_engine_mask=(1 << FE) - 1, remote_sem=T.sem.summed,
+                                   srcs=[T.land[r * NB + k] for r in range(n)],
+                                   dsts=[T.res[k * 128:(k + 1) * 128, :] for c in mine], alu_op=1)]
         g.wait_ge(T.sem.arrived, GE * n * len(blocks))
         g.remote_dma_fused(folds, local_sem=T.sem.sent)
         g.wait_ge(T.sem.sent, FE * len(folds))

@@ -2,19 +2,20 @@ from concourse.bass import DstId, RemoteDMATransfer
 
 W = 4
 PIECE = {3: (0, 128), 1: (128, 224), 2: (224, 256), 4: (256, 320)}
-START = (0, 128, 192)
+START = (0, 96, 192)
 NB = len(START)
-RES = {3: (0, 128), 1: (128, 224), 2: (224, 256), 4: (320, 384)}
+HOME = {3: 0, 1: 1, 2: 2, 4: 2}
 
 SCRATCH = {
     "pack": ("dram", [320, W], "float32"),
-    "land": ("dram", [8 * NB, 128, W], "float32"),
+    "land": ("dram", [8, 128, W], "float32"),
     "res": ("dram", [128 * NB, W], "float32"),
 }
-SEMAPHORES = ["loaded", "sent", "arrived", "summed", "stored"]
+SEMAPHORES = ["ld1", "ld2", "sent", "arrived", "sum0", "sum1", "sum2", "stored"]
 
 HELPER_CORES = (0, 4, 1)
-GE = 2
+MASK = (0x0F, 0xF0, 0xFF)
+GE = (4, 4, 8)
 FE = 16
 
 
@@ -35,42 +36,56 @@ def rank_program(g, core, T, topo):
             rid, pid = topo.addr(c, core)
             ids.append(DstId(rid=rid, pnc=pid))
         k = blocks[0]
-        folds = [RemoteDMATransfer(dst_ids=ids, dma_engine_mask=(1 << FE) - 1, remote_sem=T.sem.summed,
-                                   srcs=[T.land[r * NB + k] for r in range(n)],
-                                   dsts=[T.res[k * 128:(k + 1) * 128, :] for c in mine], alu_op=1)]
-        g.wait_ge(T.sem.arrived, GE * n * len(blocks))
-        g.remote_dma_fused(folds, local_sem=T.sem.sent)
-        g.wait_ge(T.sem.sent, FE * len(folds))
+        g.wait_ge(T.sem.arrived, GE[k] * n)
+        g.remote_dma_fused(
+            [RemoteDMATransfer(dst_ids=ids, dma_engine_mask=(1 << FE) - 1, remote_sem=T.sem["sum%d" % k],
+                               srcs=[T.land[r] for r in range(n)],
+                               dsts=[T.res[k * 128:(k + 1) * 128, :] for c in mine], alu_op=1)],
+            local_sem=T.sem.sent)
+        g.wait_ge(T.sem.sent, FE)
         return
 
     if rank is None:
         return
 
-    queue = {3: g.sync, 2: g.sync, 1: g.scalar, 4: g.scalar}
-    order = (3, 1, 4, 2)
-
-    for k in order:
+    def load(q, k, sem):
         a, b = PIECE[k]
-        queue[k].dma_start(T.pack[a:b, :], T["x%d" % k][:]).then_inc(T.sem.loaded, 16)
-    g.wait_ge(T.sem.loaded, 64)
+        q.dma_start(T.pack[a:b, :], T["x%d" % k][:]).then_inc(sem, 16)
 
-    transfers = []
+    def gather(ks):
+        transfers = []
+        for k in ks:
+            ids = []
+            for ch in sorted(chips, key=lambda ch: ch == core // 8):
+                rid, pid = topo.addr(folder(ch, k), core)
+                ids.append(DstId(rid=rid, pnc=pid))
+            transfers.append(RemoteDMATransfer(dst_ids=ids, dma_engine_mask=MASK[k], remote_sem=T.sem.arrived,
+                                               srcs=[T.pack[START[k]:START[k] + 128, :]],
+                                               dsts=[T.land[rank] for i in ids]))
+        g.remote_dma_fused(transfers, local_sem=T.sem.sent)
+
+    def store(q, k):
+        a, b = PIECE[k]
+        off = 128 * HOME[k] - START[HOME[k]]
+        q.wait_ge(T.sem["sum%d" % HOME[k]], FE)
+        q.dma_start(T["y%d" % k][:], T.res[a + off:b + off, :]).then_inc(T.sem.stored, 16)
+
+    load(g.sync, 3, T.sem.ld1)
+    load(g.scalar, 1, T.sem.ld1)
+    load(g.sync, 2, T.sem.ld2)
+    load(g.scalar, 4, T.sem.ld2)
+
+    g.wait_ge(T.sem.ld1, 32)
+    gather([0, 1])
+    g.wait_ge(T.sem.ld2, 32)
+    gather([2])
+
+    store(g.sync, 3)
+    store(g.scalar, 1)
+    store(g.sync, 2)
+    store(g.scalar, 4)
+
+    g.wait_ge(T.sem.sent, sum(GE))
     for k in range(NB):
-        ids = []
-        for ch in sorted(chips, key=lambda ch: ch == core // 8):
-            rid, pid = topo.addr(folder(ch, k), core)
-            ids.append(DstId(rid=rid, pnc=pid))
-        transfers.append(RemoteDMATransfer(dst_ids=ids, dma_engine_mask=((1 << GE) - 1) << (GE * k),
-                                           remote_sem=T.sem.arrived, srcs=[T.pack[START[k]:START[k] + 128, :]],
-                                           dsts=[T.land[rank * NB + k] for i in ids]))
-    g.remote_dma_fused(transfers, local_sem=T.sem.sent)
-
-    g.sync.wait_ge(T.sem.summed, FE * NB)
-    g.scalar.wait_ge(T.sem.summed, FE * NB)
-    for k in order:
-        a, b = RES[k]
-        queue[k].dma_start(T["y%d" % k][:], T.res[a:b, :]).then_inc(T.sem.stored, 16)
-
-    g.wait_ge(T.sem.sent, GE * NB)
-    g.wait_ge(T.sem.summed, FE * NB)
+        g.wait_ge(T.sem["sum%d" % k], FE)
     g.wait_ge(T.sem.stored, 64)

from concourse.bass import DstId, RemoteDMATransfer

W = 4
PIECE = {3: (0, 128), 1: (128, 224), 2: (224, 256), 4: (256, 320)}
START = (0, 96, 192)
NB = len(START)
HOME = {3: 0, 1: 1, 2: 2, 4: 2}

SCRATCH = {
    "pack": ("dram", [320, W], "float32"),
    "land": ("dram", [8, 128, W], "float32"),
    "res": ("dram", [128 * NB, W], "float32"),
}
SEMAPHORES = ["ld1", "ld2", "sent", "arrived", "sum0", "sum1", "sum2", "stored"]

HELPER_CORES = (0, 4, 1)
MASK = (0x0F, 0xF0, 0xFF)
GE = (4, 4, 8)
FE = 16


def rank_program(g, core, T, topo):
    cores = list(T.cores)
    n = len(cores)
    rank = T.rank_of(core)
    chips = sorted(set(c // 8 for c in cores))

    def folder(chip8, k):
        return chip8 * 8 + HELPER_CORES[k]

    blocks = [k for k in range(NB) if core // 8 in chips and folder(core // 8, k) == core]
    if blocks:
        mine = [c for c in cores if c // 8 == core // 8]
        ids = []
        for c in mine:
            rid, pid = topo.addr(c, core)
            ids.append(DstId(rid=rid, pnc=pid))
        k = blocks[0]
        g.wait_ge(T.sem.arrived, GE[k] * n)
        g.remote_dma_fused(
            [RemoteDMATransfer(dst_ids=ids, dma_engine_mask=(1 << FE) - 1, remote_sem=T.sem["sum%d" % k],
                               srcs=[T.land[r] for r in range(n)],
                               dsts=[T.res[k * 128:(k + 1) * 128, :] for c in mine], alu_op=1)],
            local_sem=T.sem.sent)
        g.wait_ge(T.sem.sent, FE)
        return

    if rank is None:
        return

    def load(q, k, sem):
        a, b = PIECE[k]
        q.dma_start(T.pack[a:b, :], T["x%d" % k][:]).then_inc(sem, 16)

    def gather(ks):
        transfers = []
        for k in ks:
            ids = []
            for ch in sorted(chips, key=lambda ch: ch == core // 8):
                rid, pid = topo.addr(folder(ch, k), core)
                ids.append(DstId(rid=rid, pnc=pid))
            transfers.append(RemoteDMATransfer(dst_ids=ids, dma_engine_mask=MASK[k], remote_sem=T.sem.arrived,
                                               srcs=[T.pack[START[k]:START[k] + 128, :]],
                                               dsts=[T.land[rank] for i in ids]))
        g.remote_dma_fused(transfers, local_sem=T.sem.sent)

    def store(q, k):
        a, b = PIECE[k]
        off = 128 * HOME[k] - START[HOME[k]]
        q.wait_ge(T.sem["sum%d" % HOME[k]], FE)
        q.dma_start(T["y%d" % k][:], T.res[a + off:b + off, :]).then_inc(T.sem.stored, 16)

    load(g.sync, 3, T.sem.ld1)
    load(g.scalar, 1, T.sem.ld1)
    load(g.sync, 2, T.sem.ld2)
    load(g.scalar, 4, T.sem.ld2)

    g.wait_ge(T.sem.ld1, 32)
    gather([0, 1])
    g.wait_ge(T.sem.ld2, 32)
    gather([2])

    store(g.sync, 3)
    store(g.scalar, 1)
    store(g.sync, 2)
    store(g.scalar, 4)

    g.wait_ge(T.sem.sent, sum(GE))
    for k in range(NB):
        g.wait_ge(T.sem["sum%d" % k], FE)
    g.wait_ge(T.sem.stored, 64)
